import numpy as np
CORES = [21,61,69,109]
N = 4
ROOT = 2
def setup_inputs(rng):
    return {"x": rng.standard_normal((N, 128, N * 1024), dtype=np.float32)}
def reference(x):
    return {"y": np.stack([x[ROOT][:, r * 1024:(r + 1) * 1024] for r in range(N)])}

@@ -1,0 +1,111 @@
+from concourse.bass import DstId, RemoteDMATransfer
+
+STAGES = [16, 16, 16, 16, 16, 16]
+WINDOW = 2
+K = len(STAGES)
+COLS = 1024
+LANE_MASK = (0x000F, 0x00F0, 0x0F00, 0xF000)
+OFF_CHIP = 0x00FF
+
+
+def _buf(lane, k):
+    return "b%d_%d" % (lane, k)
+
+
+def _arr(lane, k):
+    return "a%d_%d" % (lane, k)
+
+
+def _plan():
+    dest = {0: 21, 1: 61, 3: 109}
+    plan = {}
+    p = 0
+    for k, rows in enumerate(STAGES):
+        third = p // 32
+        blk0 = (1, 3, 0)[third]
+        relay = ((54, 55), (102, 103), (None, None))[third][k % 2]
+        plan[(0, k)] = (blk0, 96 + p - 32 * third, rows, relay, dest[blk0])
+        plan[(1, k)] = (1, p, rows, (70, 71)[k % 2], dest[1])
+        plan[(2, k)] = (3, p, rows, (66, 67)[k % 2], dest[3])
+        plan[(3, k)] = (0, p, rows, (64, 65)[k % 2], dest[0])
+        p += rows
+    return plan
+
+
+PLAN = _plan()
+
+SCRATCH = {}
+for _lane in range(4):
+    for _k in range(K):
+        SCRATCH[_buf(_lane, _k)] = ("dram", [128, STAGES[_k] * COLS // 128], "float32")
+
+SEMAPHORES = ([_arr(l, k) for l in range(4) for k in range(K)] + ["ld%d" % k for k in range(K)]
+              + ["sent", "stored", "go"])
+
+
+def _root(g, T, topo):
+    for k in range(K):
+        if k >= WINDOW:
+            g.sync.wait_ge(T.sem["ld%d" % (k - WINDOW)], 64)
+            g.scalar.wait_ge(T.sem["ld%d" % (k - WINDOW)], 64)
+        for lane in range(4):
+            blk, r0, rows, _h, _d = PLAN[(lane, k)]
+            q = g.sync if lane % 2 == 0 else g.scalar
+            q.dma_start(T[_buf(lane, k)][:], T.x[r0:r0 + rows, blk * COLS:(blk + 1) * COLS]).then_inc(
+                T.sem["ld%d" % k], 16)
+    for k in range(K):
+        g.wait_ge(T.sem["ld%d" % k], 64)
+        trs = []
+        for lane in range(4):
+            _b, _r, _n, helper, dst = PLAN[(lane, k)]
+            to = dst if helper is None else helper
+            rid, pid, _s = topo.addr(to)
+            trs.append(RemoteDMATransfer(dst_ids=[DstId(rid=rid, pnc=pid)], dma_engine_mask=LANE_MASK[lane],
+                                         remote_sem=T.sem[_arr(lane, k)],
+                                         src=T[_buf(lane, k)][:], dst=T[_buf(lane, k)][:]))
+        g.remote_dma_fused(trs, local_sem=T.sem.sent)
+    g.sem_inc(T.sem.go, 1)
+    g.scalar.wait_ge(T.sem.go, 1)
+    g.scalar.dma_start(T.y[:, :], T.x[:, 2 * COLS:3 * COLS]).then_inc(T.sem.stored, 16)
+    g.wait_ge(T.sem.sent, 16 * K)
+    g.wait_ge(T.sem.stored, 16)
+
+
+def _helper(g, core, T, topo):
+    n = 0
+    for k in range(K):
+        for lane in range(4):
+            _b, _r, _n, helper, dst = PLAN[(lane, k)]
+            if helper != core:
+                continue
+            rid, pid, _s = topo.addr(dst)
+            g.wait_ge(T.sem[_arr(lane, k)], 4)
+            g.remote_dma(T[_buf(lane, k)][:], T[_buf(lane, k)][:], T.sem[_arr(lane, k)], T.sem.sent, pid, rid,
+                         OFF_CHIP)
+            n += 1
+    if n:
+        g.wait_ge(T.sem.sent, 8 * n)
+
+
+def _receiver(g, core, T):
+    n = 0
+    for k in range(K):
+        for lane in range(4):
+            _b, r0, rows, helper, dst = PLAN[(lane, k)]
+            if dst != core:
+                continue
+            q = g.scalar if lane == 0 else g.sync
+            q.wait_ge(T.sem[_arr(lane, k)], 4 if helper is None else 8)
+            q.dma_start(T.y[r0:r0 + rows, :], T[_buf(lane, k)][:]).then_inc(T.sem.stored, 16)
+            n += 1
+    g.wait_ge(T.sem.stored, 16 * n)
+
+
+def rank_program(g, core, T, topo):
+    rank = T.rank_of(core)
+    if rank == 2:
+        _root(g, T, topo)
+    elif rank is not None:
+        _receiver(g, core, T)
+    else:
+        _helper(g, core, T, topo)

@@ -1,11 +1,19 @@
 from concourse.bass import DstId, RemoteDMATransfer
 
 STAGES = [16, 16, 16, 16, 16, 16]
-WINDOW = 2
+WINDOW_ROWS = 48
 K = len(STAGES)
 COLS = 1024
 LANE_MASK = (0x000F, 0x00F0, 0x0F00, 0xF000)
 OFF_CHIP = 0x00FF
+END = [sum(STAGES[:k + 1]) for k in range(K)]
+
+
+def _gate(k):
+    for j in range(k):
+        if END[k] - END[j] <= WINDOW_ROWS:
+            return j
+    return None if END[k] <= WINDOW_ROWS else k - 1
 
 
 def _buf(lane, k):
@@ -45,9 +53,10 @@ SEMAPHORES = ([_arr(l, k) for l in range(4) for k in range(K)] + ["ld%d" % k for
 
 def _root(g, T, topo):
     for k in range(K):
-        if k >= WINDOW:
-            g.sync.wait_ge(T.sem["ld%d" % (k - WINDOW)], 64)
-            g.scalar.wait_ge(T.sem["ld%d" % (k - WINDOW)], 64)
+        j = None if END[k] <= WINDOW_ROWS else _gate(k)
+        if j is not None:
+            g.sync.wait_ge(T.sem["ld%d" % j], 64)
+            g.scalar.wait_ge(T.sem["ld%d" % j], 64)
         for lane in range(4):
             blk, r0, rows, _h, _d = PLAN[(lane, k)]
             q = g.sync if lane % 2 == 0 else g.scalar

@@ -1,95 +1,87 @@
 from concourse.bass import DstId, RemoteDMATransfer
 
-STAGES = [16, 16, 16, 16, 16, 16]
-WINDOW_ROWS = 48
-K = len(STAGES)
 COLS = 1024
-LANE_MASK = (0x000F, 0x00F0, 0x0F00, 0xF000)
+SLOT_MASK = (0x000F, 0x00F0, 0x0F00, 0xF000)
 OFF_CHIP = 0x00FF
-END = [sum(STAGES[:k + 1]) for k in range(K)]
-
-
-def _gate(k):
-    for j in range(k):
-        if END[k] - END[j] <= WINDOW_ROWS:
-            return j
-    return None if END[k] <= WINDOW_ROWS else k - 1
-
-
-def _buf(lane, k):
-    return "b%d_%d" % (lane, k)
-
-
-def _arr(lane, k):
-    return "a%d_%d" % (lane, k)
+WINDOW = 3
+DEST = {0: 21, 1: 61, 3: 109}
 
 
 def _plan():
-    dest = {0: 21, 1: 61, 3: 109}
-    plan = {}
-    p = 0
-    for k, rows in enumerate(STAGES):
-        third = p // 32
-        blk0 = (1, 3, 0)[third]
-        relay = ((54, 55), (102, 103), (None, None))[third][k % 2]
-        plan[(0, k)] = (blk0, 96 + p - 32 * third, rows, relay, dest[blk0])
-        plan[(1, k)] = (1, p, rows, (70, 71)[k % 2], dest[1])
-        plan[(2, k)] = (3, p, rows, (66, 67)[k % 2], dest[3])
-        plan[(3, k)] = (0, p, rows, (64, 65)[k % 2], dest[0])
-        p += rows
-    return plan
+    calls = []
+    for k in range(5):
+        r3 = ((1, 80, 54), (3, 80, 102), (1, 96, 55), (3, 96, 103), (1, 112, 54))[k]
+        calls.append([(0, r3[0], r3[1], 16, r3[2]),
+                      (1, 1, 16 * k, 16, (70, 71)[k % 2]),
+                      (2, 3, 16 * k, 16, (66, 67)[k % 2]),
+                      (3, 0, 16 * k, 16, (64, 65)[k % 2])])
+    calls.append([(0, 0, 88, 8, None),
+                  (1, 3, 112, 8, 71),
+                  (2, 3, 120, 8, 67),
+                  (3, 0, 80, 8, 65)])
+    calls.append([(0, 0, 96, 16, None),
+                  (1, 0, 112, 16, None)])
+    return calls
 
 
-PLAN = _plan()
+CALLS = _plan()
+K = len(CALLS)
+
+
+def _buf(k, slot):
+    return "b%d_%d" % (k, slot)
+
+
+def _arr(k, slot):
+    return "a%d_%d" % (k, slot)
+
 
 SCRATCH = {}
-for _lane in range(4):
-    for _k in range(K):
-        SCRATCH[_buf(_lane, _k)] = ("dram", [128, STAGES[_k] * COLS // 128], "float32")
-
-SEMAPHORES = ([_arr(l, k) for l in range(4) for k in range(K)] + ["ld%d" % k for k in range(K)]
-              + ["sent", "stored", "go"])
+SEMAPHORES = ["sent", "stored", "go"]
+for _k in range(K):
+    SEMAPHORES.append("ld%d" % _k)
+    for _p in CALLS[_k]:
+        SCRATCH[_buf(_k, _p[0])] = ("dram", [128, _p[3] * COLS // 128], "float32")
+        SEMAPHORES.append(_arr(_k, _p[0]))
 
 
 def _root(g, T, topo):
     for k in range(K):
-        j = None if END[k] <= WINDOW_ROWS else _gate(k)
-        if j is not None:
-            g.sync.wait_ge(T.sem["ld%d" % j], 64)
-            g.scalar.wait_ge(T.sem["ld%d" % j], 64)
-        for lane in range(4):
-            blk, r0, rows, _h, _d = PLAN[(lane, k)]
-            q = g.sync if lane % 2 == 0 else g.scalar
-            q.dma_start(T[_buf(lane, k)][:], T.x[r0:r0 + rows, blk * COLS:(blk + 1) * COLS]).then_inc(
+        if k >= WINDOW:
+            n = 16 * len(CALLS[k - WINDOW])
+            g.sync.wait_ge(T.sem["ld%d" % (k - WINDOW)], n)
+            g.scalar.wait_ge(T.sem["ld%d" % (k - WINDOW)], n)
+        for slot, blk, r0, rows, _h in CALLS[k]:
+            q = g.sync if slot % 2 == 0 else g.scalar
+            q.dma_start(T[_buf(k, slot)][:], T.x[r0:r0 + rows, blk * COLS:(blk + 1) * COLS]).then_inc(
                 T.sem["ld%d" % k], 16)
+    total = 0
     for k in range(K):
-        g.wait_ge(T.sem["ld%d" % k], 64)
+        g.wait_ge(T.sem["ld%d" % k], 16 * len(CALLS[k]))
         trs = []
-        for lane in range(4):
-            _b, _r, _n, helper, dst = PLAN[(lane, k)]
-            to = dst if helper is None else helper
-            rid, pid, _s = topo.addr(to)
-            trs.append(RemoteDMATransfer(dst_ids=[DstId(rid=rid, pnc=pid)], dma_engine_mask=LANE_MASK[lane],
-                                         remote_sem=T.sem[_arr(lane, k)],
-                                         src=T[_buf(lane, k)][:], dst=T[_buf(lane, k)][:]))
+        for slot, blk, _r, _n, helper in CALLS[k]:
+            rid, pid, _s = topo.addr(DEST[blk] if helper is None else helper)
+            trs.append(RemoteDMATransfer(dst_ids=[DstId(rid=rid, pnc=pid)], dma_engine_mask=SLOT_MASK[slot],
+                                         remote_sem=T.sem[_arr(k, slot)],
+                                         src=T[_buf(k, slot)][:], dst=T[_buf(k, slot)][:]))
+            total += 4
         g.remote_dma_fused(trs, local_sem=T.sem.sent)
     g.sem_inc(T.sem.go, 1)
     g.scalar.wait_ge(T.sem.go, 1)
     g.scalar.dma_start(T.y[:, :], T.x[:, 2 * COLS:3 * COLS]).then_inc(T.sem.stored, 16)
-    g.wait_ge(T.sem.sent, 16 * K)
+    g.wait_ge(T.sem.sent, total)
     g.wait_ge(T.sem.stored, 16)
 
 
 def _helper(g, core, T, topo):
     n = 0
     for k in range(K):
-        for lane in range(4):
-            _b, _r, _n, helper, dst = PLAN[(lane, k)]
+        for slot, blk, _r, _n, helper in CALLS[k]:
             if helper != core:
                 continue
-            rid, pid, _s = topo.addr(dst)
-            g.wait_ge(T.sem[_arr(lane, k)], 4)
-            g.remote_dma(T[_buf(lane, k)][:], T[_buf(lane, k)][:], T.sem[_arr(lane, k)], T.sem.sent, pid, rid,
+            rid, pid, _s = topo.addr(DEST[blk])
+            g.wait_ge(T.sem[_arr(k, slot)], 4)
+            g.remote_dma(T[_buf(k, slot)][:], T[_buf(k, slot)][:], T.sem[_arr(k, slot)], T.sem.sent, pid, rid,
                          OFF_CHIP)
             n += 1
     if n:
@@ -99,13 +91,13 @@ def _helper(g, core, T, topo):
 def _receiver(g, core, T):
     n = 0
     for k in range(K):
-        for lane in range(4):
-            _b, r0, rows, helper, dst = PLAN[(lane, k)]
-            if dst != core:
+        for slot, blk, r0, rows, helper in CALLS[k]:
+            if DEST[blk] != core:
                 continue
-            q = g.scalar if lane == 0 else g.sync
-            q.wait_ge(T.sem[_arr(lane, k)], 4 if helper is None else 8)
-            q.dma_start(T.y[r0:r0 + rows, :], T[_buf(lane, k)][:]).then_inc(T.sem.stored, 16)
+            side = slot == 0 or helper is None or (k == 5 and slot == 1)
+            q = g.scalar if side else g.sync
+            q.wait_ge(T.sem[_arr(k, slot)], 4 if helper is None else 8)
+            q.dma_start(T.y[r0:r0 + rows, :], T[_buf(k, slot)][:]).then_inc(T.sem.stored, 16)
             n += 1
     g.wait_ge(T.sem.stored, 16 * n)
 

from concourse.bass import DstId, RemoteDMATransfer

COLS = 1024
SLOT_MASK = (0x000F, 0x00F0, 0x0F00, 0xF000)
OFF_CHIP = 0x00FF
WINDOW = 3
DEST = {0: 21, 1: 61, 3: 109}


def _plan():
    calls = []
    for k in range(5):
        r3 = ((1, 80, 54), (3, 80, 102), (1, 96, 55), (3, 96, 103), (1, 112, 54))[k]
        calls.append([(0, r3[0], r3[1], 16, r3[2]),
                      (1, 1, 16 * k, 16, (70, 71)[k % 2]),
                      (2, 3, 16 * k, 16, (66, 67)[k % 2]),
                      (3, 0, 16 * k, 16, (64, 65)[k % 2])])
    calls.append([(0, 0, 88, 8, None),
                  (1, 3, 112, 8, 71),
                  (2, 3, 120, 8, 67),
                  (3, 0, 80, 8, 65)])
    calls.append([(0, 0, 96, 16, None),
                  (1, 0, 112, 16, None)])
    return calls


CALLS = _plan()
K = len(CALLS)


def _buf(k, slot):
    return "b%d_%d" % (k, slot)


def _arr(k, slot):
    return "a%d_%d" % (k, slot)


SCRATCH = {}
SEMAPHORES = ["sent", "stored", "go"]
for _k in range(K):
    SEMAPHORES.append("ld%d" % _k)
    for _p in CALLS[_k]:
        SCRATCH[_buf(_k, _p[0])] = ("dram", [128, _p[3] * COLS // 128], "float32")
        SEMAPHORES.append(_arr(_k, _p[0]))


def _root(g, T, topo):
    for k in range(K):
        if k >= WINDOW:
            n = 16 * len(CALLS[k - WINDOW])
            g.sync.wait_ge(T.sem["ld%d" % (k - WINDOW)], n)
            g.scalar.wait_ge(T.sem["ld%d" % (k - WINDOW)], n)
        for slot, blk, r0, rows, _h in CALLS[k]:
            q = g.sync if slot % 2 == 0 else g.scalar
            q.dma_start(T[_buf(k, slot)][:], T.x[r0:r0 + rows, blk * COLS:(blk + 1) * COLS]).then_inc(
                T.sem["ld%d" % k], 16)
    total = 0
    for k in range(K):
        g.wait_ge(T.sem["ld%d" % k], 16 * len(CALLS[k]))
        trs = []
        for slot, blk, _r, _n, helper in CALLS[k]:
            rid, pid, _s = topo.addr(DEST[blk] if helper is None else helper)
            trs.append(RemoteDMATransfer(dst_ids=[DstId(rid=rid, pnc=pid)], dma_engine_mask=SLOT_MASK[slot],
                                         remote_sem=T.sem[_arr(k, slot)],
                                         src=T[_buf(k, slot)][:], dst=T[_buf(k, slot)][:]))
            total += 4
        g.remote_dma_fused(trs, local_sem=T.sem.sent)
    g.sem_inc(T.sem.go, 1)
    g.scalar.wait_ge(T.sem.go, 1)
    g.scalar.dma_start(T.y[:, :], T.x[:, 2 * COLS:3 * COLS]).then_inc(T.sem.stored, 16)
    g.wait_ge(T.sem.sent, total)
    g.wait_ge(T.sem.stored, 16)


def _helper(g, core, T, topo):
    n = 0
    for k in range(K):
        for slot, blk, _r, _n, helper in CALLS[k]:
            if helper != core:
                continue
            rid, pid, _s = topo.addr(DEST[blk])
            g.wait_ge(T.sem[_arr(k, slot)], 4)
            g.remote_dma(T[_buf(k, slot)][:], T[_buf(k, slot)][:], T.sem[_arr(k, slot)], T.sem.sent, pid, rid,
                         OFF_CHIP)
            n += 1
    if n:
        g.wait_ge(T.sem.sent, 8 * n)


def _receiver(g, core, T):
    n = 0
    for k in range(K):
        for slot, blk, r0, rows, helper in CALLS[k]:
            if DEST[blk] != core:
                continue
            side = slot == 0 or helper is None or (k == 5 and slot == 1)
            q = g.scalar if side else g.sync
            q.wait_ge(T.sem[_arr(k, slot)], 4 if helper is None else 8)
            q.dma_start(T.y[r0:r0 + rows, :], T[_buf(k, slot)][:]).then_inc(T.sem.stored, 16)
            n += 1
    g.wait_ge(T.sem.stored, 16 * n)


def rank_program(g, core, T, topo):
    rank = T.rank_of(core)
    if rank == 2:
        _root(g, T, topo)
    elif rank is not None:
        _receiver(g, core, T)
    else:
        _helper(g, core, T, topo)
